import numpy as np
import ml_dtypes


def mxq(x, axis, fmt="e4m3"):
    dtype, down = {"e4m3": (ml_dtypes.float8_e4m3fn, 7), "e5m2": (ml_dtypes.float8_e5m2, 14)}[fmt]
    v = np.moveaxis(np.asarray(x, np.float32).astype(ml_dtypes.bfloat16).astype(np.float64), axis, -1)
    blocks = v.reshape(v.shape[:-1] + (-1, 32))
    amax = np.abs(blocks).max(-1, keepdims=True)
    byte = np.maximum(np.where(amax > 0, np.frexp(amax)[1] - 1 + 127, 0) - down, 1)
    scale = np.exp2(byte - 127.0)
    codes = (blocks / scale).astype(np.float32).astype(dtype).astype(np.float64)
    return np.moveaxis((codes * scale).reshape(v.shape), -1, axis)


WIDE = False


def mx_kscale(k):
    if not WIDE:
        return np.ones(k)
    levels = np.array([10, -10, 5, -5, 0])
    if k % 512:
        return np.exp2(np.random.permutation(np.resize(levels, k // 32))).repeat(32)
    a = np.empty((k // 512, 16))
    for p in range(k // 512):
        a[p, :8] = np.random.permutation(np.resize(levels, 8))
        for g in range(8):
            far = levels[np.abs(levels - a[p, g]) >= 10]
            a[p, g + 8] = far[np.random.randint(len(far))]
    return np.exp2(a.ravel()).repeat(32)


def f64(x):
    return np.asarray(x).astype(np.float64)


def striped(idx):
    return np.tile(idx.reshape(-1, 16).T, (8, 1)).astype(np.uint16)


def unstriped(offs):
    return offs[:16].T.reshape(-1).astype(np.int64)


E2M1 = np.array([0.0, 0.5, 1.0, 1.5, 2.0, 3.0, 4.0, 6.0, -0.0, -0.5, -1.0, -1.5, -2.0, -3.0, -4.0, -6.0])


def pack_weight(w, fmt):
    k, n = w.shape
    w = f64(np.asarray(w, np.float32).astype(ml_dtypes.bfloat16)).reshape(k // 32, 32, n)
    amax = np.abs(w).max(1)
    if fmt == "e4m3":
        byte = np.frexp(amax)[1] - 1 + 127 - 7
    else:
        mant, ex = np.frexp(amax / 6.0)
        byte = np.where(mant > 0.5, ex, ex - 1) + 127
    byte = np.clip(np.where(amax > 0, byte, 1), 1, 254)
    scaled = (w * np.exp2(127.0 - byte)[:, None, :]).reshape(k, n).astype(np.float32)
    by_word = np.ascontiguousarray(scaled.reshape(k // 512, 128, 4, n).transpose(0, 1, 3, 2))
    if fmt == "e4m3":
        words = by_word.astype(ml_dtypes.float8_e4m3fn).view(np.uint8)
    else:
        c = by_word.astype(ml_dtypes.float4_e2m1fn).view(np.uint8) & 0xF
        words = (c[..., 0::2] | (c[..., 1::2] << 4)).reshape(k // 512, 128, 2 * n)
    return np.ascontiguousarray(words), np.ascontiguousarray(byte.astype(np.uint8).reshape(k // 512, 16, n))


def unpack_weight(words, scales, fmt):
    g, _, n = scales.shape
    words = np.ascontiguousarray(words).reshape(g, 128, n, -1)
    if fmt == "e4m3":
        vals = words.view(ml_dtypes.float8_e4m3fn).astype(np.float64)
    else:
        nib = np.empty((g, 128, n, 4), np.uint8)
        nib[..., 0::2] = words & 0xF
        nib[..., 1::2] = words >> 4
        vals = E2M1[nib]
    vals = vals * np.repeat(np.exp2(scales.astype(np.float64) - 127.0), 8, axis=1)[..., None]
    return vals.transpose(0, 1, 3, 2).reshape(g * 512, n)


def relu2(v):
    return np.maximum(v, 0.0) ** 2


K, T, E, C, H, N = 2048, 640, 6, 256, 512, 384
R = 2


def by_expert(wq, xq):
    return np.concatenate([wq[e].T @ xq[:, e * C:(e + 1) * C] for e in range(E)], axis=1)


def setup_inputs():
    n = np.random.standard_normal
    s = mx_kscale(K)[:, None]
    u = mx_kscale(H)
    slot_token = np.concatenate([r * (T // R) + np.random.permutation(T // R)[:C // R] for e in range(E) for r in range(R)])
    w1 = [pack_weight(m, "e2m1") for m in n((E, K, H)) / np.sqrt(K) / s[None] * u[None, None, :]]
    w2 = [pack_weight(m, "e2m1") for m in n((E, H, N)) / np.sqrt(H) / u[None, :, None] ** 2]
    x = pack_weight(n((K, T)) * s, "e4m3")
    return {
        "x_words": x[0],
        "x_scales": x[1],
        "w1_words": np.stack([m[0] for m in w1]),
        "w1_scales": np.stack([m[1] for m in w1]),
        "w2_words": np.stack([m[0] for m in w2]),
        "w2_scales": np.stack([m[1] for m in w2]),
        "offs": striped(slot_token),
    }


def reference(x_words, x_scales, w1_words, w1_scales, w2_words, w2_scales, offs):
    idx = unstriped(offs)
    w1 = np.stack([unpack_weight(w1_words[e], w1_scales[e], "e2m1") for e in range(E)])
    w2 = np.stack([unpack_weight(w2_words[e], w2_scales[e], "e2m1") for e in range(E)])
    xq = unpack_weight(x_words, x_scales, "e4m3")[:, idx]
    h = relu2(by_expert(w1, xq))
    y = by_expert(w2, mxq(h, 0, "e4m3"))
    return y.reshape(N, E, R, C // R).transpose(0, 2, 1, 3).reshape(N, E * C)

@@ -1,0 +1,181 @@
+from contextlib import ExitStack
+
+import concourse.mybir as mybir
+from concourse.masks import make_identity
+
+K, T, E, C, H, N = 2048, 640, 6, 256, 512, 384
+R = 2
+FLOPS = 2 * E * C * (K * H + H * N)
+
+F32 = mybir.dt.float32
+BF16 = mybir.dt.bfloat16
+I32 = mybir.dt.int32
+U32 = mybir.dt.uint32
+U16 = mybir.dt.uint16
+U8 = mybir.dt.uint8
+FP8X4 = mybir.dt.float8_e4m3fn_x4
+FP4X4 = mybir.dt.float4_e2m1fn_x4
+ACT = mybir.ActivationFunctionType
+
+P = 128
+PASSES = K // 512
+NT = N // P
+S = E * C
+FIRST = 2
+
+
+def tile_moe_pke_mlp_relu2_kernel(
+    tc, x_words, x_scales, w1_words, w1_scales, w2_words, w2_scales, offs, out
+):
+    nc = tc.nc
+    with ExitStack() as ctx:
+        keep = ctx.enter_context(tc.tile_pool(name="keep", bufs=1))
+        ring = ctx.enter_context(tc.tile_pool(name="ring", bufs=2))
+        psum = ctx.enter_context(tc.psum_pool(name="psum", bufs=1))
+
+        offsets = keep.tile([P, S // 16], U16, name="offsets")
+        nc.sync.dma_start(offsets[:], offs)
+
+        xs_win = keep.tile([P, T], U8, name="xs_win", align_bytes=64)
+        nc.sync.dma_start(xs_win[0:64, :].bitcast(I32), x_scales.rearrange("a f t -> f a t").bitcast(I32))
+        nc.vector.memset(xs_win[64:P, :].bitcast(I32), 0)
+
+        groups = [(0, FIRST), (FIRST, E)]
+        w1s = []
+        xs_planes = []
+        for g, (e0, e1) in enumerate(groups):
+            t = keep.tile([P, (e1 - e0) * PASSES * H], U8, name="w1s%d" % g, align_bytes=64)
+            (nc.vector if g == 0 else nc.gpsimd).memset(t[:].bitcast(I32), 0)
+            w1s.append(t)
+            t = keep.tile([P, PASSES * (e1 - e0) * C], U8, name="xs_planes%d" % g, align_bytes=64)
+            nc.vector.memset(t[:].bitcast(I32), 0)
+            xs_planes.append(t)
+        w2s = keep.tile([P, E * N], U8, name="w2s", align_bytes=64)
+        nc.gpsimd.memset(w2s[:].bitcast(I32), 0)
+
+        xw_first = keep.tile([P, T], I32, name="xw_first", align_bytes=64)
+        xw_rest = keep.tile([P, (PASSES - 1) * T], I32, name="xw_rest", align_bytes=64)
+        xw_hbm = x_words.rearrange("a p t r -> p a (t r)").bitcast(I32)
+        nc.sync.dma_start(xw_first[:], xw_hbm[:, 0, :])
+
+        def load_w1s(g, queue):
+            e0, e1 = groups[g]
+            src = w1_scales[e0:e1].rearrange("e a (q r) i -> r q (e a) i", r=4).bitcast(I32)
+            for r in range(4):
+                queue.dma_start(
+                    w1s[g][r:P:32, :].bitcast(I32).rearrange("q (b i) -> q b i", i=H // 4), src[r]
+                )
+
+        load_w1s(0, nc.sync)
+        nc.sync.dma_start(xw_rest[:].rearrange("p (a t) -> p a t", t=T), xw_hbm[:, 1:PASSES, :])
+
+        def load_w1(e):
+            t = ring.tile([P, PASSES * 2 * H], U8, name="w1w", align_bytes=64)
+            nc.sync.dma_start(
+                t[:].bitcast(I32).rearrange("p (a w) -> p a w", a=PASSES),
+                w1_words[e].rearrange("a p w -> p a w").bitcast(I32),
+            )
+            return t
+
+        w1w = {0: load_w1(0), 1: load_w1(1)}
+        w2w = keep.tile([P, E * 2 * N], U8, name="w2w", align_bytes=64)
+        nc.sync.dma_start(
+            w2w[:].bitcast(I32).rearrange("p (e w) -> p e w", e=E),
+            w2_words.rearrange("e a p w -> p (e a) w").bitcast(I32),
+        )
+
+        ident = keep.tile([P, P], F32, name="ident")
+        make_identity(nc, ident[:])
+        load_w1s(1, nc.gpsimd)
+        w2s_src = w2_scales.rearrange("e a (q r) n -> r q (e a) n", r=4).bitcast(I32)
+        for r in range(4):
+            nc.gpsimd.dma_start(w2s[r:P:32, :].bitcast(I32).rearrange("q (e n) -> q e n", e=E), w2s_src[r])
+
+        def gather_scales(g, queue):
+            e0, e1 = groups[g]
+            n = (e1 - e0) * C
+            got = keep.tile([P, n], U8, name="xs_got%d" % g, align_bytes=64)
+            for c0 in range(0, n, C):
+                j0 = e0 * C + c0
+                nc.vector.tensor_copy(
+                    got[:, c0 : c0 + C], xs_win[:].indirect(offsets[:, j0 // 16 : (j0 + C) // 16])
+                )
+            for q in range(4):
+                queue.dma_start(
+                    xs_planes[g][32 * q : 32 * q + 4, :].bitcast(I32).rearrange("r (a s) -> r a s", a=PASSES),
+                    got[16 * q : 16 * q + 16, :].bitcast(I32),
+                )
+
+        def gather_words(e):
+            got = []
+            for a in range(PASSES):
+                t = ring.tile([P, C], U32, name="xw_got%d" % a, align_bytes=64)
+                win = xw_first[:] if a == 0 else xw_rest[:, (a - 1) * T : a * T]
+                nc.vector.tensor_copy(
+                    t[:], win.bitcast(U32).indirect(offsets[:, e * C // 16 : (e + 1) * C // 16])
+                )
+                got.append(t)
+            return got
+
+        out_v = out.rearrange("(b p) (m e u) -> p b m e u", p=P, m=R, e=E)
+
+        gather_scales(0, nc.scalar)
+        xg = {0: gather_words(0)}
+        gather_scales(1, nc.sync)
+        for e in range(E):
+            g = 0 if e < FIRST else 1
+            e0, e1 = groups[g]
+            n = (e1 - e0) * C
+            if e + 1 < E:
+                xg[e + 1] = gather_words(e + 1)
+            hb = ring.tile([P, C * 4], BF16, name="hb", align_bytes=64)
+            relus = []
+            for m in range(R):
+                acc = psum.tile([P, H], F32, name="acc", bufs=4)
+                for a in range(PASSES):
+                    s0 = a * n + (e - e0) * C + m * P
+                    b0 = ((e - e0) * PASSES + a) * H
+                    nc.tensor.matmul_mx(
+                        out=acc[:],
+                        lhsT=xg[e][a][:, m * P : (m + 1) * P].bitcast(FP8X4),
+                        lhsT_scale=xs_planes[g][:, s0 : s0 + P],
+                        rhs=w1w[e][:, a * 2 * H : (a + 1) * 2 * H].bitcast(FP4X4),
+                        rhs_scale=w1s[g][:, b0 : b0 + H],
+                        start=(a == 0),
+                        stop=(a == PASSES - 1),
+                    )
+                rl = ring.tile([P, 4, P], F32, name="relu", bufs=4)
+                nc.scalar.activation(rl[:], acc[:].rearrange("s (q t) -> s t q", t=4), ACT.Relu)
+                relus.append(rl)
+            if e + 2 < E:
+                w1w[e + 2] = load_w1(e + 2)
+            for m in range(R):
+                tr = psum.tile([P, 4, P], F32, name="tr", bufs=2)
+                for t in range(4):
+                    nc.tensor.transpose(tr[:, t, :], relus[m][:, t, :], ident[:])
+                nc.scalar.activation(
+                    hb[:, m * 4 * P : (m + 1) * 4 * P].rearrange("q (s t) -> q s t", t=4),
+                    tr[:].rearrange("q t s -> q s t"),
+                    ACT.Square,
+                )
+            hq = ring.tile([P, C], U32, name="hq", align_bytes=64)
+            hs = ring.tile([P, C], U8, name="hs", align_bytes=64)
+            nc.vector.quantize_mx(out=hq[:].bitcast(FP8X4), scales=hs[:], in_=hb[:])
+            ya = psum.tile([P, 2, C], F32, name="ya")
+            yb = psum.tile([P, 1, C], F32, name="yb")
+            for b in range(NT):
+                dst = ya[:, b, :] if b < 2 else yb[:, 0, :]
+                nc.tensor.matmul_mx(
+                    out=dst,
+                    lhsT=w2w[:, (e * N + b * P) * 2 : (e * N + (b + 1) * P) * 2].bitcast(FP4X4),
+                    lhsT_scale=w2s[:, e * N + b * P : e * N + (b + 1) * P],
+                    rhs=hq[:].bitcast(FP8X4),
+                    rhs_scale=hs[:],
+                    start=True,
+                    stop=True,
+                )
+            stage = ring.tile([P, R, NT, P], F32, name="stage", bufs=3)
+            nc.scalar.copy(stage[:, :, 0:2, :], ya[:].rearrange("p b (m u) -> p m b u", m=R))
+            nc.vector.tensor_copy(stage[:, :, 2, :], yb[:, 0, :].rearrange("p (m u) -> p m u", m=R))
+            for m in range(R):
+                nc.sync.dma_start(out_v[:, :, m, e, :], stage[:, m, :, :])

@@ -21,7 +21,7 @@ P = 128
 PASSES = K // 512
 NT = N // P
 S = E * C
-FIRST = 2
+PAIR = 2
 
 
 def tile_moe_pke_mlp_relu2_kernel(
@@ -38,39 +38,31 @@ def tile_moe_pke_mlp_relu2_kernel(
 
         xs_win = keep.tile([P, T], U8, name="xs_win", align_bytes=64)
         nc.sync.dma_start(xs_win[0:64, :].bitcast(I32), x_scales.rearrange("a f t -> f a t").bitcast(I32))
-        nc.vector.memset(xs_win[64:P, :].bitcast(I32), 0)
 
-        groups = [(0, FIRST), (FIRST, E)]
-        w1s = []
-        xs_planes = []
-        for g, (e0, e1) in enumerate(groups):
-            t = keep.tile([P, (e1 - e0) * PASSES * H], U8, name="w1s%d" % g, align_bytes=64)
-            (nc.vector if g == 0 else nc.gpsimd).memset(t[:].bitcast(I32), 0)
-            w1s.append(t)
-            t = keep.tile([P, PASSES * (e1 - e0) * C], U8, name="xs_planes%d" % g, align_bytes=64)
-            nc.vector.memset(t[:].bitcast(I32), 0)
-            xs_planes.append(t)
+        w1s = [keep.tile([P, PAIR * PASSES * H], U8, name="w1s%d" % i, align_bytes=64) for i in range(2)]
+        xs_planes = [keep.tile([P, PASSES * PAIR * C], U8, name="xs_planes%d" % i, align_bytes=64) for i in range(2)]
         w2s = keep.tile([P, E * N], U8, name="w2s", align_bytes=64)
-        nc.gpsimd.memset(w2s[:].bitcast(I32), 0)
+        nc.vector.memset(w1s[0][:].bitcast(I32), 0)
+        nc.vector.memset(w1s[1][:].bitcast(I32), 0)
+        nc.vector.memset(xs_win[64:P, :].bitcast(I32), 0)
+        nc.vector.memset(xs_planes[0][:].bitcast(I32), 0)
 
-        xw_first = keep.tile([P, T], I32, name="xw_first", align_bytes=64)
-        xw_rest = keep.tile([P, (PASSES - 1) * T], I32, name="xw_rest", align_bytes=64)
         xw_hbm = x_words.rearrange("a p t r -> p a (t r)").bitcast(I32)
-        nc.sync.dma_start(xw_first[:], xw_hbm[:, 0, :])
+        xw_win = []
+        for h in range(2):
+            t = keep.tile([P, 2 * T], I32, name="xw_win%d" % h, align_bytes=64)
+            nc.sync.dma_start(t[:].rearrange("p (a t) -> p a t", t=T), xw_hbm[:, 2 * h : 2 * h + 2, :])
+            xw_win.append(t)
 
         def load_w1s(g, queue):
-            e0, e1 = groups[g]
-            src = w1_scales[e0:e1].rearrange("e a (q r) i -> r q (e a) i", r=4).bitcast(I32)
+            src = w1_scales[PAIR * g : PAIR * (g + 1)].rearrange("e a (q r) i -> r q (e a) i", r=4).bitcast(I32)
             for r in range(4):
                 queue.dma_start(
-                    w1s[g][r:P:32, :].bitcast(I32).rearrange("q (b i) -> q b i", i=H // 4), src[r]
+                    w1s[g % 2][r:P:32, :].bitcast(I32).rearrange("q (b i) -> q b i", i=H // 4), src[r]
                 )
 
-        load_w1s(0, nc.sync)
-        nc.sync.dma_start(xw_rest[:].rearrange("p (a t) -> p a t", t=T), xw_hbm[:, 1:PASSES, :])
-
         def load_w1(e):
-            t = ring.tile([P, PASSES * 2 * H], U8, name="w1w", align_bytes=64)
+            t = keep.tile([P, PASSES * 2 * H], U8, name="w1w%d" % e, tag="w1_slot%d" % (e % 3), align_bytes=64)
             nc.sync.dma_start(
                 t[:].bitcast(I32).rearrange("p (a w) -> p a w", a=PASSES),
                 w1_words[e].rearrange("a p w -> p a w").bitcast(I32),
@@ -78,39 +70,35 @@ def tile_moe_pke_mlp_relu2_kernel(
             return t
 
         w1w = {0: load_w1(0), 1: load_w1(1)}
-        w2w = keep.tile([P, E * 2 * N], U8, name="w2w", align_bytes=64)
-        nc.sync.dma_start(
-            w2w[:].bitcast(I32).rearrange("p (e w) -> p e w", e=E),
-            w2_words.rearrange("e a p w -> p (e a) w").bitcast(I32),
-        )
+        load_w1s(0, nc.scalar)
+        load_w1s(1, nc.sync)
 
         ident = keep.tile([P, P], F32, name="ident")
         make_identity(nc, ident[:])
-        load_w1s(1, nc.gpsimd)
-        w2s_src = w2_scales.rearrange("e a (q r) n -> r q (e a) n", r=4).bitcast(I32)
-        for r in range(4):
-            nc.gpsimd.dma_start(w2s[r:P:32, :].bitcast(I32).rearrange("q (e n) -> q e n", e=E), w2s_src[r])
 
-        def gather_scales(g, queue):
-            e0, e1 = groups[g]
-            n = (e1 - e0) * C
-            got = keep.tile([P, n], U8, name="xs_got%d" % g, align_bytes=64)
-            for c0 in range(0, n, C):
-                j0 = e0 * C + c0
+        def gather_scales(g, tag, queue):
+            got = keep.tile([P, PAIR * C], U8, name="xs_got%d" % g, tag=tag, align_bytes=64)
+            for c0 in range(0, PAIR * C, C):
+                j0 = PAIR * g * C + c0
                 nc.vector.tensor_copy(
                     got[:, c0 : c0 + C], xs_win[:].indirect(offsets[:, j0 // 16 : (j0 + C) // 16])
                 )
             for q in range(4):
                 queue.dma_start(
-                    xs_planes[g][32 * q : 32 * q + 4, :].bitcast(I32).rearrange("r (a s) -> r a s", a=PASSES),
+                    xs_planes[g % 2][32 * q : 32 * q + 4, :].bitcast(I32).rearrange("r (a s) -> r a s", a=PASSES),
                     got[16 * q : 16 * q + 16, :].bitcast(I32),
                 )
 
         def gather_words(e):
             got = []
             for a in range(PASSES):
-                t = ring.tile([P, C], U32, name="xw_got%d" % a, align_bytes=64)
-                win = xw_first[:] if a == 0 else xw_rest[:, (a - 1) * T : a * T]
+                if e == 1 and a == PASSES - 1:
+                    t = keep.tile([P, C], U32, name="xw_got_relay", tag="relay_c", align_bytes=64)
+                elif a == 0:
+                    t = keep.tile([P, C], U32, name="xw_got0_%d" % e, tag="pass0_%d" % (e % 2), align_bytes=64)
+                else:
+                    t = ring.tile([P, C], U32, name="xw_got%d" % a, align_bytes=64)
+                win = xw_win[a // 2][:, (a % 2) * T : (a % 2 + 1) * T]
                 nc.vector.tensor_copy(
                     t[:], win.bitcast(U32).indirect(offsets[:, e * C // 16 : (e + 1) * C // 16])
                 )
@@ -119,63 +107,115 @@ def tile_moe_pke_mlp_relu2_kernel(
 
         out_v = out.rearrange("(b p) (m e u) -> p b m e u", p=P, m=R, e=E)
 
-        gather_scales(0, nc.scalar)
-        xg = {0: gather_words(0)}
-        gather_scales(1, nc.sync)
-        for e in range(E):
-            g = 0 if e < FIRST else 1
-            e0, e1 = groups[g]
-            n = (e1 - e0) * C
-            if e + 1 < E:
-                xg[e + 1] = gather_words(e + 1)
-            hb = ring.tile([P, C * 4], BF16, name="hb", align_bytes=64)
-            relus = []
+        gather_scales(0, "w1_slot2", nc.scalar)
+        nc.vector.memset(xs_planes[1][:].bitcast(I32), 0)
+        gather_scales(1, "got_b", nc.sync)
+        xg = {0: gather_words(0), 1: gather_words(1)}
+
+        w1w[2] = load_w1(2)
+        nc.vector.memset(w2s[:].bitcast(I32), 0)
+        w2s_src = w2_scales.rearrange("e a (q r) n -> r q (e a) n", r=4).bitcast(I32)
+        for r in range(4):
+            nc.sync.dma_start(w2s[r:P:32, :].bitcast(I32).rearrange("q (e n) -> q e n", e=E), w2s_src[r])
+        w2w = keep.tile([P, E * 2 * N], U8, name="w2w", tag="got_b", align_bytes=64)
+        nc.sync.dma_start(
+            w2w[:].bitcast(I32).rearrange("p (e w) -> p e w", e=E),
+            w2_words.rearrange("e a p w -> p (e a) w").bitcast(I32),
+        )
+
+        relus = {}
+
+        def first_layer(e):
+            g = e // PAIR
             for m in range(R):
                 acc = psum.tile([P, H], F32, name="acc", bufs=4)
                 for a in range(PASSES):
-                    s0 = a * n + (e - e0) * C + m * P
-                    b0 = ((e - e0) * PASSES + a) * H
+                    s0 = a * PAIR * C + (e % PAIR) * C + m * P
+                    b0 = ((e % PAIR) * PASSES + a) * H
                     nc.tensor.matmul_mx(
                         out=acc[:],
                         lhsT=xg[e][a][:, m * P : (m + 1) * P].bitcast(FP8X4),
-                        lhsT_scale=xs_planes[g][:, s0 : s0 + P],
+                        lhsT_scale=xs_planes[g % 2][:, s0 : s0 + P],
                         rhs=w1w[e][:, a * 2 * H : (a + 1) * 2 * H].bitcast(FP4X4),
-                        rhs_scale=w1s[g][:, b0 : b0 + H],
+                        rhs_scale=w1s[g % 2][:, b0 : b0 + H],
                         start=(a == 0),
                         stop=(a == PASSES - 1),
                     )
                 rl = ring.tile([P, 4, P], F32, name="relu", bufs=4)
                 nc.scalar.activation(rl[:], acc[:].rearrange("s (q t) -> s t q", t=4), ACT.Relu)
-                relus.append(rl)
+                relus[e, m] = rl
+
+        def refill(e):
+            if e + 3 < E:
+                w1w[e + 3] = load_w1(e + 3)
             if e + 2 < E:
-                w1w[e + 2] = load_w1(e + 2)
-            for m in range(R):
-                tr = psum.tile([P, 4, P], F32, name="tr", bufs=2)
-                for t in range(4):
-                    nc.tensor.transpose(tr[:, t, :], relus[m][:, t, :], ident[:])
-                nc.scalar.activation(
-                    hb[:, m * 4 * P : (m + 1) * 4 * P].rearrange("q (s t) -> q s t", t=4),
-                    tr[:].rearrange("q t s -> q s t"),
-                    ACT.Square,
-                )
-            hq = ring.tile([P, C], U32, name="hq", align_bytes=64)
+                xg[e + 2] = gather_words(e + 2)
+            if e == 1:
+                gather_scales(2, "relay_c", nc.sync)
+                load_w1s(2, nc.sync)
+
+        def hidden(e, m, hb):
+            tr = psum.tile([P, 4, P], F32, name="tr", bufs=2)
+            for t in range(4):
+                nc.tensor.transpose(tr[:, t, :], relus[e, m][:, t, :], ident[:])
+            nc.scalar.activation(hb.rearrange("q (s t) -> q s t", t=4), tr[:].rearrange("q t s -> q s t"), ACT.Square)
+
+        def product(dst, e, b, hq, hs):
+            nc.tensor.matmul_mx(
+                out=dst,
+                lhsT=w2w[:, (e * N + b * P) * 2 : (e * N + (b + 1) * P) * 2].bitcast(FP4X4),
+                lhsT_scale=w2s[:, e * N + b * P : e * N + (b + 1) * P],
+                rhs=hq.bitcast(FP8X4),
+                rhs_scale=hs,
+                start=True,
+                stop=True,
+            )
+
+        def second_layer(e, hb):
+            hq = keep.tile([P, C], U32, name="hq%d" % e, tag="pass0_%d" % ((e + 1) % 2), align_bytes=64)
             hs = ring.tile([P, C], U8, name="hs", align_bytes=64)
             nc.vector.quantize_mx(out=hq[:].bitcast(FP8X4), scales=hs[:], in_=hb[:])
             ya = psum.tile([P, 2, C], F32, name="ya")
             yb = psum.tile([P, 1, C], F32, name="yb")
             for b in range(NT):
-                dst = ya[:, b, :] if b < 2 else yb[:, 0, :]
-                nc.tensor.matmul_mx(
-                    out=dst,
-                    lhsT=w2w[:, (e * N + b * P) * 2 : (e * N + (b + 1) * P) * 2].bitcast(FP4X4),
-                    lhsT_scale=w2s[:, e * N + b * P : e * N + (b + 1) * P],
-                    rhs=hq[:].bitcast(FP8X4),
-                    rhs_scale=hs[:],
-                    start=True,
-                    stop=True,
-                )
+                product(ya[:, b, :] if b < 2 else yb[:, 0, :], e, b, hq[:], hs[:])
             stage = ring.tile([P, R, NT, P], F32, name="stage", bufs=3)
-            nc.scalar.copy(stage[:, :, 0:2, :], ya[:].rearrange("p b (m u) -> p m b u", m=R))
-            nc.vector.tensor_copy(stage[:, :, 2, :], yb[:, 0, :].rearrange("p (m u) -> p m u", m=R))
+            wide = (stage[:, :, 0:2, :], ya[:].rearrange("p b (m u) -> p m b u", m=R))
+            narrow = (stage[:, :, 2, :], yb[:, 0, :].rearrange("p (m u) -> p m u", m=R))
+            if e < 3:
+                nc.scalar.copy(*wide)
+                nc.vector.tensor_copy(*narrow)
+            else:
+                nc.vector.tensor_copy(*wide)
+                nc.vector.tensor_copy(*narrow)
             for m in range(R):
                 nc.sync.dma_start(out_v[:, :, m, e, :], stage[:, m, :, :])
+
+        def last_second_layer(e, m, hb):
+            hq = ring.tile([P, P], U32, name="hq_last", align_bytes=64)
+            hs = ring.tile([P, P], U8, name="hs_last", align_bytes=64)
+            nc.vector.quantize_mx(out=hq[:].bitcast(FP8X4), scales=hs[:], in_=hb[:])
+            ya = psum.tile([P, 2, P], F32, name="ya_last", tag="acc", bufs=4)
+            yb = psum.tile([P, P], F32, name="yb_last", tag="acc", bufs=4)
+            for b in range(NT):
+                product(ya[:, b, :] if b < 2 else yb[:], e, b, hq[:], hs[:])
+            stage = ring.tile([P, NT, P], F32, name="stage_last")
+            nc.scalar.copy(stage[:, 0:2, :], ya[:])
+            nc.vector.tensor_copy(stage[:, 2, :], yb[:])
+            nc.sync.dma_start(out_v[:, :, m, e, :], stage[:])
+
+        hb = None
+        for e in range(E):
+            first_layer(e)
+            if e > 0:
+                second_layer(e - 1, hb)
+            refill(e)
+            if e < E - 1:
+                hb = ring.tile([P, C * 4], BF16, name="hb", align_bytes=64)
+                for m in range(R):
+                    hidden(e, m, hb[:, m * 4 * P : (m + 1) * 4 * P])
+        halves = [ring.tile([P, 4 * P], BF16, name="hb_last", align_bytes=64) for m in range(R)]
+        for m in range(R):
+            hidden(E - 1, m, halves[m][:])
+        for m in range(R):
+            last_second_layer(E - 1, m, halves[m])

@@ -22,6 +22,8 @@ PASSES = K // 512
 NT = N // P
 S = E * C
 PAIR = 2
+WIN = 704
+GROUPS = ((0, PAIR), (PAIR, E))
 
 
 def tile_moe_pke_mlp_relu2_kernel(
@@ -36,16 +38,21 @@ def tile_moe_pke_mlp_relu2_kernel(
         offsets = keep.tile([P, S // 16], U16, name="offsets")
         nc.sync.dma_start(offsets[:], offs)
 
-        xs_win = keep.tile([P, T], U8, name="xs_win", align_bytes=64)
-        nc.sync.dma_start(xs_win[0:64, :].bitcast(I32), x_scales.rearrange("a f t -> f a t").bitcast(I32))
+        xs_win = keep.tile([P, WIN + 4], U8, name="xs_win", align_bytes=64)
+        nc.sync.dma_start(xs_win[0:64, 0:T].bitcast(I32), x_scales.rearrange("a f t -> f a t").bitcast(I32))
 
-        w1s = [keep.tile([P, PAIR * PASSES * H], U8, name="w1s%d" % i, align_bytes=64) for i in range(2)]
-        xs_planes = [keep.tile([P, PASSES * PAIR * C], U8, name="xs_planes%d" % i, align_bytes=64) for i in range(2)]
+        w1s_first = keep.tile([P, PAIR * PASSES * H], U8, name="w1s_first", align_bytes=64)
+        xs_planes = [
+            keep.tile([P, PASSES * (e1 - e0) * C + 4], U8, name="xs_planes%d" % e0, align_bytes=64)
+            for e0, e1 in GROUPS
+        ]
         w2s = keep.tile([P, E * N], U8, name="w2s", align_bytes=64)
-        nc.vector.memset(w1s[0][:].bitcast(I32), 0)
-        nc.vector.memset(w1s[1][:].bitcast(I32), 0)
+        nc.gpsimd.memset(w1s_first[:].bitcast(I32), 0)
+        nc.gpsimd.memset(w2s[:].bitcast(I32), 0)
         nc.vector.memset(xs_win[64:P, :].bitcast(I32), 0)
+        nc.vector.memset(xs_win[0:64, T:].bitcast(I32), 0)
         nc.vector.memset(xs_planes[0][:].bitcast(I32), 0)
+        nc.vector.memset(xs_planes[1][:].bitcast(I32), 0)
 
         xw_hbm = x_words.rearrange("a p t r -> p a (t r)").bitcast(I32)
         xw_win = []
@@ -61,40 +68,47 @@ def tile_moe_pke_mlp_relu2_kernel(
                     w1s[g % 2][r:P:32, :].bitcast(I32).rearrange("q (b i) -> q b i", i=H // 4), src[r]
                 )
 
-        def load_w1(e):
-            t = keep.tile([P, PASSES * 2 * H], U8, name="w1w%d" % e, tag="w1_slot%d" % (e % 3), align_bytes=64)
+        def load_w1(e, dst):
             nc.sync.dma_start(
-                t[:].bitcast(I32).rearrange("p (a w) -> p a w", a=PASSES),
+                dst.bitcast(I32).rearrange("p (a w) -> p a w", a=PASSES),
                 w1_words[e].rearrange("a p w -> p a w").bitcast(I32),
             )
-            return t
+            return dst
 
-        w1w = {0: load_w1(0), 1: load_w1(1)}
+        def w1_tile(e, tag):
+            return keep.tile([P, PASSES * 2 * H], U8, name="w1w%d" % e, tag=tag, align_bytes=64)
+
+        w1w_first = w1_tile(0, "w1_first")
+        w1s = [w1s_first, w1w_first]
+        w1w = {0: load_w1(0, w1w_first[:])}
         load_w1s(0, nc.scalar)
-        load_w1s(1, nc.sync)
+        w2s_src = w2_scales.rearrange("e a (q r) n -> r q (e a) n", r=4).bitcast(I32)
+        for r in range(4):
+            nc.sync.dma_start(w2s[r:P:32, :].bitcast(I32).rearrange("q (e n) -> q e n", e=E), w2s_src[r])
 
         ident = keep.tile([P, P], F32, name="ident")
         make_identity(nc, ident[:])
 
         def gather_scales(g, tag, queue):
-            got = keep.tile([P, PAIR * C], U8, name="xs_got%d" % g, tag=tag, align_bytes=64)
-            for c0 in range(0, PAIR * C, C):
-                j0 = PAIR * g * C + c0
+            e0, e1 = GROUPS[g]
+            n = (e1 - e0) * C
+            got = keep.tile([P, n], U8, name="xs_got%d" % g, tag=tag, align_bytes=64)
+            for c0 in range(0, n, PAIR * C):
+                j0 = e0 * C + c0
                 nc.vector.tensor_copy(
-                    got[:, c0 : c0 + C], xs_win[:].indirect(offsets[:, j0 // 16 : (j0 + C) // 16])
+                    got[:, c0 : c0 + PAIR * C],
+                    xs_win[:, 0:WIN].indirect(offsets[:, j0 // 16 : (j0 + PAIR * C) // 16]),
                 )
             for q in range(4):
                 queue.dma_start(
-                    xs_planes[g % 2][32 * q : 32 * q + 4, :].bitcast(I32).rearrange("r (a s) -> r a s", a=PASSES),
+                    xs_planes[g][32 * q : 32 * q + 4, 0 : PASSES * n].bitcast(I32).rearrange("r (a s) -> r a s", a=PASSES),
                     got[16 * q : 16 * q + 16, :].bitcast(I32),
                 )
 
         def gather_words(e):
             got = []
             for a in range(PASSES):
-                if e == 1 and a == PASSES - 1:
-                    t = keep.tile([P, C], U32, name="xw_got_relay", tag="relay_c", align_bytes=64)
-                elif a == 0:
+                if a == 0:
                     t = keep.tile([P, C], U32, name="xw_got0_%d" % e, tag="pass0_%d" % (e % 2), align_bytes=64)
                 else:
                     t = ring.tile([P, C], U32, name="xw_got%d" % a, align_bytes=64)
@@ -107,52 +121,53 @@ def tile_moe_pke_mlp_relu2_kernel(
 
         out_v = out.rearrange("(b p) (m e u) -> p b m e u", p=P, m=R, e=E)
 
-        gather_scales(0, "w1_slot2", nc.scalar)
-        nc.vector.memset(xs_planes[1][:].bitcast(I32), 0)
-        gather_scales(1, "got_b", nc.sync)
+        gather_scales(0, "got_a", nc.scalar)
+        gather_scales(1, "w1_even", nc.sync)
         xg = {0: gather_words(0), 1: gather_words(1)}
 
-        w1w[2] = load_w1(2)
-        nc.vector.memset(w2s[:].bitcast(I32), 0)
-        w2s_src = w2_scales.rearrange("e a (q r) n -> r q (e a) n", r=4).bitcast(I32)
-        for r in range(4):
-            nc.sync.dma_start(w2s[r:P:32, :].bitcast(I32).rearrange("q (e n) -> q e n", e=E), w2s_src[r])
-        w2w = keep.tile([P, E * 2 * N], U8, name="w2w", tag="got_b", align_bytes=64)
+        late = keep.tile([P, PASSES * 2 * H + E * 2 * N], U8, name="late", tag="got_a", align_bytes=64)
+        w2w = late[:, PASSES * 2 * H :]
+        w1w[1] = load_w1(1, late[:, 0 : PASSES * 2 * H])
         nc.sync.dma_start(
-            w2w[:].bitcast(I32).rearrange("p (e w) -> p e w", e=E),
+            w2w.bitcast(I32).rearrange("p (e w) -> p e w", e=E),
             w2_words.rearrange("e a p w -> p (e a) w").bitcast(I32),
         )
+        w1w[2] = load_w1(2, w1_tile(2, "w1_even")[:])
 
         relus = {}
 
         def first_layer(e):
             g = e // PAIR
+            gx = min(g, 1)
+            e0, e1 = GROUPS[gx]
             for m in range(R):
                 acc = psum.tile([P, H], F32, name="acc", bufs=4)
                 for a in range(PASSES):
-                    s0 = a * PAIR * C + (e % PAIR) * C + m * P
+                    s0 = (a * (e1 - e0) + e - e0) * C + m * P
                     b0 = ((e % PAIR) * PASSES + a) * H
                     nc.tensor.matmul_mx(
                         out=acc[:],
                         lhsT=xg[e][a][:, m * P : (m + 1) * P].bitcast(FP8X4),
-                        lhsT_scale=xs_planes[g % 2][:, s0 : s0 + P],
+                        lhsT_scale=xs_planes[gx][:, s0 : s0 + P],
                         rhs=w1w[e][:, a * 2 * H : (a + 1) * 2 * H].bitcast(FP4X4),
                         rhs_scale=w1s[g % 2][:, b0 : b0 + H],
                         start=(a == 0),
                         stop=(a == PASSES - 1),
                     )
-                rl = ring.tile([P, 4, P], F32, name="relu", bufs=4)
+                if (e, m) == (0, 0):
+                    rl = keep.tile([P, 4, P], F32, name="relu_first", tag="w1_odd", align_bytes=64)
+                else:
+                    rl = ring.tile([P, 4, P], F32, name="relu", bufs=4)
                 nc.scalar.activation(rl[:], acc[:].rearrange("s (q t) -> s t q", t=4), ACT.Relu)
                 relus[e, m] = rl
 
         def refill(e):
-            if e + 3 < E:
-                w1w[e + 3] = load_w1(e + 3)
+            if e < 2:
+                load_w1s(e + 1, nc.sync)
+            if e in (2, 3):
+                w1w[e + 2] = load_w1(e + 2, w1_tile(e + 2, "w1_even" if e == 2 else "w1_odd")[:])
             if e + 2 < E:
                 xg[e + 2] = gather_words(e + 2)
-            if e == 1:
-                gather_scales(2, "relay_c", nc.sync)
-                load_w1s(2, nc.sync)
 
         def hidden(e, m, hb):
             tr = psum.tile([P, 4, P], F32, name="tr", bufs=2)
@@ -214,6 +229,8 @@ def tile_moe_pke_mlp_relu2_kernel(
                 hb = ring.tile([P, C * 4], BF16, name="hb", align_bytes=64)
                 for m in range(R):
                     hidden(e, m, hb[:, m * 4 * P : (m + 1) * 4 * P])
+            if e == 0:
+                w1w[3] = load_w1(3, w1_tile(3, "w1_odd")[:])
         halves = [ring.tile([P, 4 * P], BF16, name="hb_last", align_bytes=64) for m in range(R)]
         for m in range(R):
             hidden(E - 1, m, halves[m][:])

@@ -18,12 +18,19 @@ FP4X4 = mybir.dt.float4_e2m1fn_x4
 ACT = mybir.ActivationFunctionType
 
 P = 128
-PASSES = K // 512
+PACK = 4
+QUADS = 4
+ROWS = 4
+PASSES = K // (P * PACK)
 NT = N // P
 S = E * C
 PAIR = 2
-WIN = 704
+W1_BYTES = PASSES * 2 * H
+XS_ROWS = PASSES * QUADS * ROWS
+XS_WINDOW = 704
+ODD = 4
 GROUPS = ((0, PAIR), (PAIR, E))
+VECTOR_FREE = 3
 
 
 def tile_moe_pke_mlp_relu2_kernel(
@@ -38,37 +45,36 @@ def tile_moe_pke_mlp_relu2_kernel(
         offsets = keep.tile([P, S // 16], U16, name="offsets")
         nc.sync.dma_start(offsets[:], offs)
 
-        xs_win = keep.tile([P, WIN + 4], U8, name="xs_win", align_bytes=64)
-        nc.sync.dma_start(xs_win[0:64, 0:T].bitcast(I32), x_scales.rearrange("a f t -> f a t").bitcast(I32))
+        xs_win = keep.tile([P, XS_WINDOW + ODD], U8, name="xs_win", align_bytes=64)
+        nc.sync.dma_start(xs_win[0:XS_ROWS, 0:T].bitcast(I32), x_scales.rearrange("a f t -> f a t").bitcast(I32))
 
-        w1s_first = keep.tile([P, PAIR * PASSES * H], U8, name="w1s_first", align_bytes=64)
+        w1s_first = keep.tile([P, W1_BYTES], U8, name="w1s_first", align_bytes=64)
         xs_planes = [
-            keep.tile([P, PASSES * (e1 - e0) * C + 4], U8, name="xs_planes%d" % e0, align_bytes=64)
+            keep.tile([P, PASSES * (e1 - e0) * C + ODD], U8, name="xs_planes%d" % e0, align_bytes=64)
             for e0, e1 in GROUPS
         ]
         w2s = keep.tile([P, E * N], U8, name="w2s", align_bytes=64)
         nc.gpsimd.memset(w1s_first[:].bitcast(I32), 0)
         nc.gpsimd.memset(w2s[:].bitcast(I32), 0)
-        nc.vector.memset(xs_win[64:P, :].bitcast(I32), 0)
-        nc.vector.memset(xs_win[0:64, T:].bitcast(I32), 0)
+        nc.vector.memset(xs_win[XS_ROWS:P, :].bitcast(I32), 0)
+        nc.vector.memset(xs_win[0:XS_ROWS, T:].bitcast(I32), 0)
         nc.vector.memset(xs_planes[0][:].bitcast(I32), 0)
         nc.vector.memset(xs_planes[1][:].bitcast(I32), 0)
 
         xw_hbm = x_words.rearrange("a p t r -> p a (t r)").bitcast(I32)
-        xw_win = []
-        for h in range(2):
-            t = keep.tile([P, 2 * T], I32, name="xw_win%d" % h, align_bytes=64)
-            nc.sync.dma_start(t[:].rearrange("p (a t) -> p a t", t=T), xw_hbm[:, 2 * h : 2 * h + 2, :])
-            xw_win.append(t)
+        xw_win = [keep.tile([P, 2 * T], I32, name="xw_win%d" % d, align_bytes=64) for d in range(PASSES // 2)]
 
-        def load_w1s(g, queue):
-            src = w1_scales[PAIR * g : PAIR * (g + 1)].rearrange("e a (q r) i -> r q (e a) i", r=4).bitcast(I32)
-            for r in range(4):
+        def load_words(d):
+            nc.sync.dma_start(xw_win[d][:].rearrange("p (a t) -> p a t", t=T), xw_hbm[:, 2 * d : 2 * d + 2, :])
+
+        def load_w1_planes(pair, queue):
+            src = w1_scales[PAIR * pair : PAIR * (pair + 1)].rearrange("e a (q r) i -> r q (e a) i", r=ROWS).bitcast(I32)
+            for r in range(ROWS):
                 queue.dma_start(
-                    w1s[g % 2][r:P:32, :].bitcast(I32).rearrange("q (b i) -> q b i", i=H // 4), src[r]
+                    w1s[pair % 2][r:P:32, :].bitcast(I32).rearrange("q (c i) -> q c i", i=H // 4), src[r]
                 )
 
-        def load_w1(e, dst):
+        def load_w1_words(e, dst):
             nc.sync.dma_start(
                 dst.bitcast(I32).rearrange("p (a w) -> p a w", a=PASSES),
                 w1_words[e].rearrange("a p w -> p a w").bitcast(I32),
@@ -76,48 +82,51 @@ def tile_moe_pke_mlp_relu2_kernel(
             return dst
 
         def w1_tile(e, tag):
-            return keep.tile([P, PASSES * 2 * H], U8, name="w1w%d" % e, tag=tag, align_bytes=64)
+            return keep.tile([P, W1_BYTES], U8, name="w1w%d" % e, tag=tag, align_bytes=64)
 
         w1w_first = w1_tile(0, "w1_first")
         w1s = [w1s_first, w1w_first]
-        w1w = {0: load_w1(0, w1w_first[:])}
-        load_w1s(0, nc.scalar)
-        w2s_src = w2_scales.rearrange("e a (q r) n -> r q (e a) n", r=4).bitcast(I32)
-        for r in range(4):
+        load_words(0)
+        w1w = {0: load_w1_words(0, w1w_first[:])}
+        load_words(1)
+        load_w1_planes(0, nc.scalar)
+        w2s_src = w2_scales.rearrange("e a (q r) n -> r q (e a) n", r=ROWS).bitcast(I32)
+        for r in range(ROWS):
             nc.sync.dma_start(w2s[r:P:32, :].bitcast(I32).rearrange("q (e n) -> q e n", e=E), w2s_src[r])
 
         ident = keep.tile([P, P], F32, name="ident")
         make_identity(nc, ident[:])
 
-        def gather_scales(g, tag, queue):
-            e0, e1 = GROUPS[g]
-            n = (e1 - e0) * C
-            got = keep.tile([P, n], U8, name="xs_got%d" % g, tag=tag, align_bytes=64)
-            for c0 in range(0, n, PAIR * C):
+        def gather_scales(group, tag, queue):
+            e0, e1 = GROUPS[group]
+            width = (e1 - e0) * C
+            gathered = keep.tile([P, width], U8, name="xs_got%d" % group, tag=tag, align_bytes=64)
+            for c0 in range(0, width, PAIR * C):
                 j0 = e0 * C + c0
                 nc.vector.tensor_copy(
-                    got[:, c0 : c0 + PAIR * C],
-                    xs_win[:, 0:WIN].indirect(offsets[:, j0 // 16 : (j0 + PAIR * C) // 16]),
+                    gathered[:, c0 : c0 + PAIR * C],
+                    xs_win[:, 0:XS_WINDOW].indirect(offsets[:, j0 // 16 : (j0 + PAIR * C) // 16]),
                 )
-            for q in range(4):
+            for q in range(QUADS):
+                rows = xs_planes[group][32 * q : 32 * q + ROWS, 0 : PASSES * width]
                 queue.dma_start(
-                    xs_planes[g][32 * q : 32 * q + 4, 0 : PASSES * n].bitcast(I32).rearrange("r (a s) -> r a s", a=PASSES),
-                    got[16 * q : 16 * q + 16, :].bitcast(I32),
+                    rows.bitcast(I32).rearrange("r (a s) -> r a s", a=PASSES),
+                    gathered[16 * q : 16 * q + 16, :].bitcast(I32),
                 )
 
         def gather_words(e):
-            got = []
+            tiles = []
             for a in range(PASSES):
                 if a == 0:
-                    t = keep.tile([P, C], U32, name="xw_got0_%d" % e, tag="pass0_%d" % (e % 2), align_bytes=64)
+                    words = keep.tile([P, C], U32, name="xw_got0_%d" % e, tag="pass0_%d" % (e % 2), align_bytes=64)
                 else:
-                    t = ring.tile([P, C], U32, name="xw_got%d" % a, align_bytes=64)
+                    words = ring.tile([P, C], U32, name="xw_got%d" % a, align_bytes=64)
                 win = xw_win[a // 2][:, (a % 2) * T : (a % 2 + 1) * T]
                 nc.vector.tensor_copy(
-                    t[:], win.bitcast(U32).indirect(offsets[:, e * C // 16 : (e + 1) * C // 16])
+                    words[:], win.bitcast(U32).indirect(offsets[:, e * C // 16 : (e + 1) * C // 16])
                 )
-                got.append(t)
-            return got
+                tiles.append(words)
+            return tiles
 
         out_v = out.rearrange("(b p) (m e u) -> p b m e u", p=P, m=R, e=E)
 
@@ -125,91 +134,89 @@ def tile_moe_pke_mlp_relu2_kernel(
         gather_scales(1, "w1_even", nc.sync)
         xg = {0: gather_words(0), 1: gather_words(1)}
 
-        late = keep.tile([P, PASSES * 2 * H + E * 2 * N], U8, name="late", tag="got_a", align_bytes=64)
-        w2w = late[:, PASSES * 2 * H :]
-        w1w[1] = load_w1(1, late[:, 0 : PASSES * 2 * H])
+        late = keep.tile([P, W1_BYTES + E * 2 * N], U8, name="late", tag="got_a", align_bytes=64)
+        w2w = late[:, W1_BYTES:]
+        w1w[1] = load_w1_words(1, late[:, 0:W1_BYTES])
         nc.sync.dma_start(
             w2w.bitcast(I32).rearrange("p (e w) -> p e w", e=E),
             w2_words.rearrange("e a p w -> p (e a) w").bitcast(I32),
         )
-        w1w[2] = load_w1(2, w1_tile(2, "w1_even")[:])
+        w1w[2] = load_w1_words(2, w1_tile(2, "w1_even")[:])
 
         relus = {}
 
         def first_layer(e):
-            g = e // PAIR
-            gx = min(g, 1)
-            e0, e1 = GROUPS[gx]
-            for m in range(R):
-                acc = psum.tile([P, H], F32, name="acc", bufs=4)
-                for a in range(PASSES):
-                    s0 = (a * (e1 - e0) + e - e0) * C + m * P
-                    b0 = ((e % PAIR) * PASSES + a) * H
-                    nc.tensor.matmul_mx(
-                        out=acc[:],
-                        lhsT=xg[e][a][:, m * P : (m + 1) * P].bitcast(FP8X4),
-                        lhsT_scale=xs_planes[gx][:, s0 : s0 + P],
-                        rhs=w1w[e][:, a * 2 * H : (a + 1) * 2 * H].bitcast(FP4X4),
-                        rhs_scale=w1s[g % 2][:, b0 : b0 + H],
-                        start=(a == 0),
-                        stop=(a == PASSES - 1),
-                    )
-                if (e, m) == (0, 0):
-                    rl = keep.tile([P, 4, P], F32, name="relu_first", tag="w1_odd", align_bytes=64)
-                else:
-                    rl = ring.tile([P, 4, P], F32, name="relu", bufs=4)
-                nc.scalar.activation(rl[:], acc[:].rearrange("s (q t) -> s t q", t=4), ACT.Relu)
-                relus[e, m] = rl
+            pair = e // PAIR
+            group = min(pair, 1)
+            e0, e1 = GROUPS[group]
+            acc = [psum.tile([P, H], F32, name="acc", bufs=4) for m in range(R)]
+            order = [(m, 0) for m in range(R)] + [(m, a) for m in range(R) for a in range(1, PASSES)]
+            for m, a in order:
+                s0 = (a * (e1 - e0) + e - e0) * C + m * P
+                i0 = ((e % PAIR) * PASSES + a) * H
+                nc.tensor.matmul_mx(
+                    out=acc[m][:],
+                    lhsT=xg[e][a][:, m * P : (m + 1) * P].bitcast(FP8X4),
+                    lhsT_scale=xs_planes[group][:, s0 : s0 + P],
+                    rhs=w1w[e][:, a * 2 * H : (a + 1) * 2 * H].bitcast(FP4X4),
+                    rhs_scale=w1s[pair % 2][:, i0 : i0 + H],
+                    start=(a == 0),
+                    stop=(a == PASSES - 1),
+                )
+                if a == PASSES - 1:
+                    if (e, m) == (0, 0):
+                        relu = keep.tile([P, PACK, P], F32, name="relu_first", tag="w1_odd", align_bytes=64)
+                    else:
+                        relu = ring.tile([P, PACK, P], F32, name="relu", bufs=4)
+                    nc.scalar.activation(relu[:], acc[m][:].rearrange("s (p t) -> s t p", t=PACK), ACT.Relu)
+                    relus[e, m] = relu
 
         def refill(e):
-            if e < 2:
-                load_w1s(e + 1, nc.sync)
-            if e in (2, 3):
-                w1w[e + 2] = load_w1(e + 2, w1_tile(e + 2, "w1_even" if e == 2 else "w1_odd")[:])
+            if e < PAIR:
+                load_w1_planes(e + 1, nc.sync)
+            if PAIR <= e < E - 2:
+                w1w[e + 2] = load_w1_words(e + 2, w1_tile(e + 2, ("w1_even", "w1_odd")[e % 2])[:])
             if e + 2 < E:
                 xg[e + 2] = gather_words(e + 2)
 
-        def hidden(e, m, hb):
-            tr = psum.tile([P, 4, P], F32, name="tr", bufs=2)
-            for t in range(4):
-                nc.tensor.transpose(tr[:, t, :], relus[e, m][:, t, :], ident[:])
-            nc.scalar.activation(hb.rearrange("q (s t) -> q s t", t=4), tr[:].rearrange("q t s -> q s t"), ACT.Square)
+        def hidden(e, m, dst):
+            turned = psum.tile([P, PACK, P], F32, name="tr", bufs=2)
+            for t in range(PACK):
+                nc.tensor.transpose(turned[:, t, :], relus[e, m][:, t, :], ident[:])
+            nc.scalar.activation(
+                dst.rearrange("p (s t) -> p s t", t=PACK), turned[:].rearrange("p t s -> p s t"), ACT.Square
+            )
 
-        def product(dst, e, b, hq, hs):
+        def product(dst, e, b, codes, plane):
             nc.tensor.matmul_mx(
                 out=dst,
                 lhsT=w2w[:, (e * N + b * P) * 2 : (e * N + (b + 1) * P) * 2].bitcast(FP4X4),
                 lhsT_scale=w2s[:, e * N + b * P : e * N + (b + 1) * P],
-                rhs=hq.bitcast(FP8X4),
-                rhs_scale=hs,
+                rhs=codes.bitcast(FP8X4),
+                rhs_scale=plane,
                 start=True,
                 stop=True,
             )
 
-        def second_layer(e, hb):
+        def second_layer(e, h_bf16):
             hq = keep.tile([P, C], U32, name="hq%d" % e, tag="pass0_%d" % ((e + 1) % 2), align_bytes=64)
             hs = ring.tile([P, C], U8, name="hs", align_bytes=64)
-            nc.vector.quantize_mx(out=hq[:].bitcast(FP8X4), scales=hs[:], in_=hb[:])
+            nc.vector.quantize_mx(out=hq[:].bitcast(FP8X4), scales=hs[:], in_=h_bf16[:])
             ya = psum.tile([P, 2, C], F32, name="ya")
             yb = psum.tile([P, 1, C], F32, name="yb")
             for b in range(NT):
                 product(ya[:, b, :] if b < 2 else yb[:, 0, :], e, b, hq[:], hs[:])
             stage = ring.tile([P, R, NT, P], F32, name="stage", bufs=3)
-            wide = (stage[:, :, 0:2, :], ya[:].rearrange("p b (m u) -> p m b u", m=R))
-            narrow = (stage[:, :, 2, :], yb[:, 0, :].rearrange("p (m u) -> p m u", m=R))
-            if e < 3:
-                nc.scalar.copy(*wide)
-                nc.vector.tensor_copy(*narrow)
-            else:
-                nc.vector.tensor_copy(*wide)
-                nc.vector.tensor_copy(*narrow)
+            copy_wide = nc.scalar.copy if e < VECTOR_FREE else nc.vector.tensor_copy
+            copy_wide(stage[:, :, 0:2, :], ya[:].rearrange("p b (m u) -> p m b u", m=R))
+            nc.vector.tensor_copy(stage[:, :, 2, :], yb[:, 0, :].rearrange("p (m u) -> p m u", m=R))
             for m in range(R):
                 nc.sync.dma_start(out_v[:, :, m, e, :], stage[:, m, :, :])
 
-        def last_second_layer(e, m, hb):
+        def last_second_layer(e, m, h_bf16):
             hq = ring.tile([P, P], U32, name="hq_last", align_bytes=64)
             hs = ring.tile([P, P], U8, name="hs_last", align_bytes=64)
-            nc.vector.quantize_mx(out=hq[:].bitcast(FP8X4), scales=hs[:], in_=hb[:])
+            nc.vector.quantize_mx(out=hq[:].bitcast(FP8X4), scales=hs[:], in_=h_bf16[:])
             ya = psum.tile([P, 2, P], F32, name="ya_last", tag="acc", bufs=4)
             yb = psum.tile([P, P], F32, name="yb_last", tag="acc", bufs=4)
             for b in range(NT):
@@ -219,19 +226,19 @@ def tile_moe_pke_mlp_relu2_kernel(
             nc.vector.tensor_copy(stage[:, 2, :], yb[:])
             nc.sync.dma_start(out_v[:, :, m, e, :], stage[:])
 
-        hb = None
+        hb = {}
         for e in range(E):
             first_layer(e)
             if e > 0:
-                second_layer(e - 1, hb)
+                second_layer(e - 1, hb[e - 1])
             refill(e)
             if e < E - 1:
-                hb = ring.tile([P, C * 4], BF16, name="hb", align_bytes=64)
+                hb[e] = ring.tile([P, C * PACK], BF16, name="hb", align_bytes=64)
                 for m in range(R):
-                    hidden(e, m, hb[:, m * 4 * P : (m + 1) * 4 * P])
+                    hidden(e, m, hb[e][:, m * PACK * P : (m + 1) * PACK * P])
             if e == 0:
-                w1w[3] = load_w1(3, w1_tile(3, "w1_odd")[:])
-        halves = [ring.tile([P, 4 * P], BF16, name="hb_last", align_bytes=64) for m in range(R)]
+                w1w[3] = load_w1_words(3, w1_tile(3, "w1_odd")[:])
+        halves = [ring.tile([P, PACK * P], BF16, name="hb_last", align_bytes=64) for m in range(R)]
         for m in range(R):
             hidden(E - 1, m, halves[m][:])
         for m in range(R):

from contextlib import ExitStack

import concourse.mybir as mybir
from concourse.masks import make_identity

K, T, E, C, H, N = 2048, 640, 6, 256, 512, 384
R = 2
FLOPS = 2 * E * C * (K * H + H * N)

F32 = mybir.dt.float32
BF16 = mybir.dt.bfloat16
I32 = mybir.dt.int32
U32 = mybir.dt.uint32
U16 = mybir.dt.uint16
U8 = mybir.dt.uint8
FP8X4 = mybir.dt.float8_e4m3fn_x4
FP4X4 = mybir.dt.float4_e2m1fn_x4
ACT = mybir.ActivationFunctionType

P = 128
PACK = 4
QUADS = 4
ROWS = 4
PASSES = K // (P * PACK)
NT = N // P
S = E * C
PAIR = 2
W1_BYTES = PASSES * 2 * H
XS_ROWS = PASSES * QUADS * ROWS
XS_WINDOW = 704
ODD = 4
GROUPS = ((0, PAIR), (PAIR, E))
VECTOR_FREE = 3


def tile_moe_pke_mlp_relu2_kernel(
    tc, x_words, x_scales, w1_words, w1_scales, w2_words, w2_scales, offs, out
):
    nc = tc.nc
    with ExitStack() as ctx:
        keep = ctx.enter_context(tc.tile_pool(name="keep", bufs=1))
        ring = ctx.enter_context(tc.tile_pool(name="ring", bufs=2))
        psum = ctx.enter_context(tc.psum_pool(name="psum", bufs=1))

        offsets = keep.tile([P, S // 16], U16, name="offsets")
        nc.sync.dma_start(offsets[:], offs)

        xs_win = keep.tile([P, XS_WINDOW + ODD], U8, name="xs_win", align_bytes=64)
        nc.sync.dma_start(xs_win[0:XS_ROWS, 0:T].bitcast(I32), x_scales.rearrange("a f t -> f a t").bitcast(I32))

        w1s_first = keep.tile([P, W1_BYTES], U8, name="w1s_first", align_bytes=64)
        xs_planes = [
            keep.tile([P, PASSES * (e1 - e0) * C + ODD], U8, name="xs_planes%d" % e0, align_bytes=64)
            for e0, e1 in GROUPS
        ]
        w2s = keep.tile([P, E * N], U8, name="w2s", align_bytes=64)
        nc.gpsimd.memset(w1s_first[:].bitcast(I32), 0)
        nc.gpsimd.memset(w2s[:].bitcast(I32), 0)
        nc.vector.memset(xs_win[XS_ROWS:P, :].bitcast(I32), 0)
        nc.vector.memset(xs_win[0:XS_ROWS, T:].bitcast(I32), 0)
        nc.vector.memset(xs_planes[0][:].bitcast(I32), 0)
        nc.vector.memset(xs_planes[1][:].bitcast(I32), 0)

        xw_hbm = x_words.rearrange("a p t r -> p a (t r)").bitcast(I32)
        xw_win = [keep.tile([P, 2 * T], I32, name="xw_win%d" % d, align_bytes=64) for d in range(PASSES // 2)]

        def load_words(d):
            nc.sync.dma_start(xw_win[d][:].rearrange("p (a t) -> p a t", t=T), xw_hbm[:, 2 * d : 2 * d + 2, :])

        def load_w1_planes(pair, queue):
            src = w1_scales[PAIR * pair : PAIR * (pair + 1)].rearrange("e a (q r) i -> r q (e a) i", r=ROWS).bitcast(I32)
            for r in range(ROWS):
                queue.dma_start(
                    w1s[pair % 2][r:P:32, :].bitcast(I32).rearrange("q (c i) -> q c i", i=H // 4), src[r]
                )

        def load_w1_words(e, dst):
            nc.sync.dma_start(
                dst.bitcast(I32).rearrange("p (a w) -> p a w", a=PASSES),
                w1_words[e].rearrange("a p w -> p a w").bitcast(I32),
            )
            return dst

        def w1_tile(e, tag):
            return keep.tile([P, W1_BYTES], U8, name="w1w%d" % e, tag=tag, align_bytes=64)

        w1w_first = w1_tile(0, "w1_first")
        w1s = [w1s_first, w1w_first]
        load_words(0)
        w1w = {0: load_w1_words(0, w1w_first[:])}
        load_words(1)
        load_w1_planes(0, nc.scalar)
        w2s_src = w2_scales.rearrange("e a (q r) n -> r q (e a) n", r=ROWS).bitcast(I32)
        for r in range(ROWS):
            nc.sync.dma_start(w2s[r:P:32, :].bitcast(I32).rearrange("q (e n) -> q e n", e=E), w2s_src[r])

        ident = keep.tile([P, P], F32, name="ident")
        make_identity(nc, ident[:])

        def gather_scales(group, tag, queue):
            e0, e1 = GROUPS[group]
            width = (e1 - e0) * C
            gathered = keep.tile([P, width], U8, name="xs_got%d" % group, tag=tag, align_bytes=64)
            for c0 in range(0, width, PAIR * C):
                j0 = e0 * C + c0
                nc.vector.tensor_copy(
                    gathered[:, c0 : c0 + PAIR * C],
                    xs_win[:, 0:XS_WINDOW].indirect(offsets[:, j0 // 16 : (j0 + PAIR * C) // 16]),
                )
            for q in range(QUADS):
                rows = xs_planes[group][32 * q : 32 * q + ROWS, 0 : PASSES * width]
                queue.dma_start(
                    rows.bitcast(I32).rearrange("r (a s) -> r a s", a=PASSES),
                    gathered[16 * q : 16 * q + 16, :].bitcast(I32),
                )

        def gather_words(e):
            tiles = []
            for a in range(PASSES):
                if a == 0:
                    words = keep.tile([P, C], U32, name="xw_got0_%d" % e, tag="pass0_%d" % (e % 2), align_bytes=64)
                else:
                    words = ring.tile([P, C], U32, name="xw_got%d" % a, align_bytes=64)
                win = xw_win[a // 2][:, (a % 2) * T : (a % 2 + 1) * T]
                nc.vector.tensor_copy(
                    words[:], win.bitcast(U32).indirect(offsets[:, e * C // 16 : (e + 1) * C // 16])
                )
                tiles.append(words)
            return tiles

        out_v = out.rearrange("(b p) (m e u) -> p b m e u", p=P, m=R, e=E)

        gather_scales(0, "got_a", nc.scalar)
        gather_scales(1, "w1_even", nc.sync)
        xg = {0: gather_words(0), 1: gather_words(1)}

        late = keep.tile([P, W1_BYTES + E * 2 * N], U8, name="late", tag="got_a", align_bytes=64)
        w2w = late[:, W1_BYTES:]
        w1w[1] = load_w1_words(1, late[:, 0:W1_BYTES])
        nc.sync.dma_start(
            w2w.bitcast(I32).rearrange("p (e w) -> p e w", e=E),
            w2_words.rearrange("e a p w -> p (e a) w").bitcast(I32),
        )
        w1w[2] = load_w1_words(2, w1_tile(2, "w1_even")[:])

        relus = {}

        def first_layer(e):
            pair = e // PAIR
            group = min(pair, 1)
            e0, e1 = GROUPS[group]
            acc = [psum.tile([P, H], F32, name="acc", bufs=4) for m in range(R)]
            order = [(m, 0) for m in range(R)] + [(m, a) for m in range(R) for a in range(1, PASSES)]
            for m, a in order:
                s0 = (a * (e1 - e0) + e - e0) * C + m * P
                i0 = ((e % PAIR) * PASSES + a) * H
                nc.tensor.matmul_mx(
                    out=acc[m][:],
                    lhsT=xg[e][a][:, m * P : (m + 1) * P].bitcast(FP8X4),
                    lhsT_scale=xs_planes[group][:, s0 : s0 + P],
                    rhs=w1w[e][:, a * 2 * H : (a + 1) * 2 * H].bitcast(FP4X4),
                    rhs_scale=w1s[pair % 2][:, i0 : i0 + H],
                    start=(a == 0),
                    stop=(a == PASSES - 1),
                )
                if a == PASSES - 1:
                    if (e, m) == (0, 0):
                        relu = keep.tile([P, PACK, P], F32, name="relu_first", tag="w1_odd", align_bytes=64)
                    else:
                        relu = ring.tile([P, PACK, P], F32, name="relu", bufs=4)
                    nc.scalar.activation(relu[:], acc[m][:].rearrange("s (p t) -> s t p", t=PACK), ACT.Relu)
                    relus[e, m] = relu

        def refill(e):
            if e < PAIR:
                load_w1_planes(e + 1, nc.sync)
            if PAIR <= e < E - 2:
                w1w[e + 2] = load_w1_words(e + 2, w1_tile(e + 2, ("w1_even", "w1_odd")[e % 2])[:])
            if e + 2 < E:
                xg[e + 2] = gather_words(e + 2)

        def hidden(e, m, dst):
            turned = psum.tile([P, PACK, P], F32, name="tr", bufs=2)
            for t in range(PACK):
                nc.tensor.transpose(turned[:, t, :], relus[e, m][:, t, :], ident[:])
            nc.scalar.activation(
                dst.rearrange("p (s t) -> p s t", t=PACK), turned[:].rearrange("p t s -> p s t"), ACT.Square
            )

        def product(dst, e, b, codes, plane):
            nc.tensor.matmul_mx(
                out=dst,
                lhsT=w2w[:, (e * N + b * P) * 2 : (e * N + (b + 1) * P) * 2].bitcast(FP4X4),
                lhsT_scale=w2s[:, e * N + b * P : e * N + (b + 1) * P],
                rhs=codes.bitcast(FP8X4),
                rhs_scale=plane,
                start=True,
                stop=True,
            )

        def second_layer(e, h_bf16):
            hq = keep.tile([P, C], U32, name="hq%d" % e, tag="pass0_%d" % ((e + 1) % 2), align_bytes=64)
            hs = ring.tile([P, C], U8, name="hs", align_bytes=64)
            nc.vector.quantize_mx(out=hq[:].bitcast(FP8X4), scales=hs[:], in_=h_bf16[:])
            ya = psum.tile([P, 2, C], F32, name="ya")
            yb = psum.tile([P, 1, C], F32, name="yb")
            for b in range(NT):
                product(ya[:, b, :] if b < 2 else yb[:, 0, :], e, b, hq[:], hs[:])
            stage = ring.tile([P, R, NT, P], F32, name="stage", bufs=3)
            copy_wide = nc.scalar.copy if e < VECTOR_FREE else nc.vector.tensor_copy
            copy_wide(stage[:, :, 0:2, :], ya[:].rearrange("p b (m u) -> p m b u", m=R))
            nc.vector.tensor_copy(stage[:, :, 2, :], yb[:, 0, :].rearrange("p (m u) -> p m u", m=R))
            for m in range(R):
                nc.sync.dma_start(out_v[:, :, m, e, :], stage[:, m, :, :])

        def last_second_layer(e, m, h_bf16):
            hq = ring.tile([P, P], U32, name="hq_last", align_bytes=64)
            hs = ring.tile([P, P], U8, name="hs_last", align_bytes=64)
            nc.vector.quantize_mx(out=hq[:].bitcast(FP8X4), scales=hs[:], in_=h_bf16[:])
            ya = psum.tile([P, 2, P], F32, name="ya_last", tag="acc", bufs=4)
            yb = psum.tile([P, P], F32, name="yb_last", tag="acc", bufs=4)
            for b in range(NT):
                product(ya[:, b, :] if b < 2 else yb[:], e, b, hq[:], hs[:])
            stage = ring.tile([P, NT, P], F32, name="stage_last")
            nc.scalar.copy(stage[:, 0:2, :], ya[:])
            nc.vector.tensor_copy(stage[:, 2, :], yb[:])
            nc.sync.dma_start(out_v[:, :, m, e, :], stage[:])

        hb = {}
        for e in range(E):
            first_layer(e)
            if e > 0:
                second_layer(e - 1, hb[e - 1])
            refill(e)
            if e < E - 1:
                hb[e] = ring.tile([P, C * PACK], BF16, name="hb", align_bytes=64)
                for m in range(R):
                    hidden(e, m, hb[e][:, m * PACK * P : (m + 1) * PACK * P])
            if e == 0:
                w1w[3] = load_w1_words(3, w1_tile(3, "w1_odd")[:])
        halves = [ring.tile([P, PACK * P], BF16, name="hb_last", align_bytes=64) for m in range(R)]
        for m in range(R):
            hidden(E - 1, m, halves[m][:])
        for m in range(R):
            last_second_layer(E - 1, m, halves[m])
